import numpy as np
import ml_dtypes


def mxq(x, axis, fmt="e4m3"):
    dtype, down = {"e4m3": (ml_dtypes.float8_e4m3fn, 7), "e5m2": (ml_dtypes.float8_e5m2, 14)}[fmt]
    v = np.moveaxis(np.asarray(x, np.float32).astype(ml_dtypes.bfloat16).astype(np.float64), axis, -1)
    blocks = v.reshape(v.shape[:-1] + (-1, 32))
    amax = np.abs(blocks).max(-1, keepdims=True)
    byte = np.maximum(np.where(amax > 0, np.frexp(amax)[1] - 1 + 127, 0) - down, 1)
    scale = np.exp2(byte - 127.0)
    codes = (blocks / scale).astype(np.float32).astype(dtype).astype(np.float64)
    return np.moveaxis((codes * scale).reshape(v.shape), -1, axis)


WIDE = False


def mx_kscale(k):
    if not WIDE:
        return np.ones(k)
    levels = np.array([10, -10, 5, -5, 0])
    if k % 512:
        return np.exp2(np.random.permutation(np.resize(levels, k // 32))).repeat(32)
    a = np.empty((k // 512, 16))
    for p in range(k // 512):
        a[p, :8] = np.random.permutation(np.resize(levels, 8))
        for g in range(8):
            far = levels[np.abs(levels - a[p, g]) >= 10]
            a[p, g + 8] = far[np.random.randint(len(far))]
    return np.exp2(a.ravel()).repeat(32)


def f64(x):
    return np.asarray(x).astype(np.float64)


def striped(idx):
    return np.tile(idx.reshape(-1, 16).T, (8, 1)).astype(np.uint16)


def unstriped(offs):
    return offs[:16].T.reshape(-1).astype(np.int64)


E2M1 = np.array([0.0, 0.5, 1.0, 1.5, 2.0, 3.0, 4.0, 6.0, -0.0, -0.5, -1.0, -1.5, -2.0, -3.0, -4.0, -6.0])


def pack_weight(w, fmt):
    k, n = w.shape
    w = f64(np.asarray(w, np.float32).astype(ml_dtypes.bfloat16)).reshape(k // 32, 32, n)
    amax = np.abs(w).max(1)
    if fmt == "e4m3":
        byte = np.frexp(amax)[1] - 1 + 127 - 7
    else:
        mant, ex = np.frexp(amax / 6.0)
        byte = np.where(mant > 0.5, ex, ex - 1) + 127
    byte = np.clip(np.where(amax > 0, byte, 1), 1, 254)
    scaled = (w * np.exp2(127.0 - byte)[:, None, :]).reshape(k, n).astype(np.float32)
    by_word = np.ascontiguousarray(scaled.reshape(k // 512, 128, 4, n).transpose(0, 1, 3, 2))
    if fmt == "e4m3":
        words = by_word.astype(ml_dtypes.float8_e4m3fn).view(np.uint8)
    else:
        c = by_word.astype(ml_dtypes.float4_e2m1fn).view(np.uint8) & 0xF
        words = (c[..., 0::2] | (c[..., 1::2] << 4)).reshape(k // 512, 128, 2 * n)
    return np.ascontiguousarray(words), np.ascontiguousarray(byte.astype(np.uint8).reshape(k // 512, 16, n))


def unpack_weight(words, scales, fmt):
    g, _, n = scales.shape
    words = np.ascontiguousarray(words).reshape(g, 128, n, -1)
    if fmt == "e4m3":
        vals = words.view(ml_dtypes.float8_e4m3fn).astype(np.float64)
    else:
        nib = np.empty((g, 128, n, 4), np.uint8)
        nib[..., 0::2] = words & 0xF
        nib[..., 1::2] = words >> 4
        vals = E2M1[nib]
    vals = vals * np.repeat(np.exp2(scales.astype(np.float64) - 127.0), 8, axis=1)[..., None]
    return vals.transpose(0, 1, 3, 2).reshape(g * 512, n)


def gelu(v):
    return 0.5 * v * (1.0 + np.tanh(np.sqrt(2.0 / np.pi) * (v + 0.044715 * v**3)))


K, K1, K2, T, S, S2 = 1024, 512, 512, 2048, 512, 1024

def setup_inputs():
    n = np.random.standard_normal
    s = mx_kscale(K)[:, None]
    d = {}
    d["tab_words"], d["tab_scales"] = pack_weight(n((K, T)) * s, "e4m3")
    d["offs"] = striped(np.random.permutation(T)[:S])
    d["offs2"] = striped(np.random.permutation(T)[:S2])
    d["w1"] = (2.2 / K * n((K1, K)) / s[:K1] / s.T).astype(np.float32)
    d["w4_words"], d["w4_scales"] = pack_weight(2.2 / K * n((K2, K)) / s[K1:] / s.T, "e2m1")
    d["bias"] = (0.8 * n(S2)).astype(np.float32)
    d["near"] = (0.7 * np.exp(0.6 * n((S2, S)))).astype(np.float32)
    return d

def reference(tab_words, tab_scales, offs, offs2, w1, w4_words, w4_scales, bias, near):
    TW = unpack_weight(tab_words, tab_scales, "e4m3")
    v = TW[:, unstriped(offs)]
    v2 = TW[:, unstriped(offs2)]
    w1q = mxq(f64(w1), 0, "e4m3")
    w4 = unpack_weight(w4_words, w4_scales, "e2m1")
    lin = w1q.T @ v[:K1] + w4.T @ v[K1:]
    h = np.maximum(lin, 0.0)
    hq = mxq(h, 0, "e4m3")
    e = v2.T @ hq
    shifted = e + f64(bias)[:, None]
    sev = np.square(shifted) + f64(near)
    return np.sqrt(sev)

@@ -1,0 +1,219 @@
+from contextlib import ExitStack
+
+import concourse.mybir as mybir
+from concourse.masks import make_identity
+
+F32 = mybir.dt.float32
+BF16 = mybir.dt.bfloat16
+I32 = mybir.dt.int32
+U32 = mybir.dt.uint32
+U16 = mybir.dt.uint16
+U8 = mybir.dt.uint8
+FP8X4 = mybir.dt.float8_e4m3fn_x4
+FP4X4 = mybir.dt.float4_e2m1fn_x4
+ACT = mybir.ActivationFunctionType
+ALU = mybir.AluOpType
+
+P = 128
+K = 1024
+T = 2048
+S = 512
+S2 = 1024
+FLOPS = 2 * K * K * S + 2 * K * S2 * S
+
+PLANE = (12, 0)
+SCALE_LOADS = ((0, 12, 16), (12, 44, 0), (44, 68, 4), (68, 100, 0), (100, 128, 4))
+
+
+def tile_list_street_name_confusion_kernel(
+    tc, tab_words, tab_scales, offs, offs2, w1, w4_words, w4_scales, bias, near, out
+):
+    nc = tc.nc
+    with ExitStack() as ctx:
+        sb = ctx.enter_context(tc.tile_pool(name="sb", bufs=1))
+        ps = ctx.enter_context(tc.psum_pool(name="ps", bufs=1))
+
+        def sbuf(name, shape, dtype, tag=None):
+            return sb.tile(shape, dtype, name=name, tag=tag or name, align_bytes=64)
+
+        def bank(i, name, shape):
+            return ps.tile(shape, F32, name=name, tag="bank%d" % i)
+
+        idx = sb.tile([P, S // 16], U16, name="idx")
+        idx2 = sb.tile([P, S2 // 16], U16, name="idx2")
+        tabw = [sbuf("tabw%d" % a, [P, T], U32) for a in range(2)]
+        tabs = sbuf("tabs", [P, T], U8)
+        w4raw = sbuf("w4raw", [P, 2 * K], U8)
+        w4sraw = sbuf("w4sraw", [P, K], U8)
+        w1raw = [sbuf("w1raw0", [P, 4, 512], F32), sbuf("w1raw1", [P, 4, 256], F32), sbuf("w1raw2", [P, 4, 256], F32)]
+        near_sb = [sbuf("near%d" % g, [P, 2, S], F32) for g in range(4)]
+        bias_rows = sbuf("bias_rows", [P, P], F32)
+        ident = sbuf("ident", [P, P], F32)
+        zero_in = sbuf("zero_in", [P, 1], F32)
+        zero = sbuf("zero", [P, 1], F32)
+
+        def load_words(a):
+            nc.sync.dma_start(tabw[a][:].bitcast(I32), tab_words[a].rearrange("p t i -> p (t i)").bitcast(I32))
+
+        w1v = w1.rearrange("(p j) c -> p j c", j=4)
+        scale_rows = tab_scales.rearrange("a q t -> (a q) t").bitcast(I32)
+
+        nc.vector.memset(bias_rows[:], 0.0)
+        nc.scalar.dma_start(bias_rows[0:8, :], bias.rearrange("(c p) -> c p", p=P))
+        nc.vector.memset(w4sraw[:].bitcast(I32), 0)
+        nc.vector.memset(zero_in[:], 0.0)
+        load_words(1)
+        nc.sync.dma_start(w4raw[:].bitcast(I32), w4_words[0].bitcast(I32))
+        nc.sync.dma_start(idx[:], offs)
+        for p0, p1, r0 in SCALE_LOADS:
+            nc.scalar.dma_start(tabs[p0:p1, :].bitcast(I32), scale_rows[r0 : r0 + p1 - p0, :])
+        for q in range(4):
+            nc.scalar.dma_start(w4sraw[32 * q : 32 * q + 4, :].bitcast(I32), w4_scales[0, 4 * q : 4 * q + 4, :].bitcast(I32))
+        nc.sync.dma_start(w1raw[0][:], w1v[:, :, 0:512])
+        nc.sync.dma_start(idx2[:], offs2)
+        load_words(0)
+        nc.sync.dma_start(w1raw[1][:], w1v[:, :, 512:768])
+        nc.sync.dma_start(w1raw[2][:], w1v[:, :, 768:1024])
+        for g in range(4):
+            nc.sync.dma_start(near_sb[g][:], near[256 * g : 256 * (g + 1), :].rearrange("(c p) j -> p c j", p=P))
+
+        nc.scalar.activation(zero[:], zero_in[:], ACT.Sqrt)
+        make_identity(nc, ident[:])
+        bias_ps = bank(7, "bias_ps", [P, P])
+        nc.tensor.transpose(bias_ps[:], bias_rows[:], ident[:])
+        bias_col = sbuf("bias_col", [P, 8], F32)
+        nc.scalar.copy(bias_col[:], bias_ps[:, 0:8])
+
+        w4d = sbuf("w4d", [P, 4, 256, 2], U8)
+        w4sd = sbuf("w4sd", [P, 4, 256], U8)
+        nc.vector.tensor_copy(
+            w4d[:].rearrange("p t q e -> p q t e"), w4raw[:].rearrange("p (q t e) -> p q t e", t=4, e=2)
+        )
+        vw = [sbuf("vw%d" % a, [P, S], U32) for a in range(2)]
+        vs = sbuf("vs", [P, S], U8)
+
+        def gather2(dst, src, lo, n):
+            nc.vector.tensor_copy(dst, src[:].indirect(idx2[:, lo // 16 : (lo + n) // 16]))
+
+        nc.vector.tensor_copy(vw[1][:], tabw[1][:].indirect(idx[:]))
+        nc.vector.tensor_copy(vs[:], tabs[:].indirect(idx[:]))
+        nc.vector.tensor_copy(w4sd[:].rearrange("p t q -> p q t"), w4sraw[:].rearrange("p (q t) -> p q t", t=4))
+
+        lin = [[bank(4 * b + jq, "lin%d%d" % (b, jq), [P, 4, P]) for jq in range(4)] for b in range(2)]
+        for b in range(2):
+            for t in range(4):
+                for jq in range(4):
+                    nc.tensor.matmul_mx(
+                        lin[b][jq][:, t, :],
+                        lhsT=w4d[:, t, P * b : P * (b + 1), :].rearrange("p q e -> p (q e)").bitcast(FP4X4),
+                        lhsT_scale=w4sd[:, t, P * b : P * (b + 1)],
+                        rhs=vw[1][:, P * jq : P * (jq + 1)].bitcast(FP8X4),
+                        rhs_scale=vs[PLANE[1] :, P * jq : P * (jq + 1)],
+                        start=(t == 0),
+                        stop=False,
+                    )
+
+        w1g = [sbuf("w1g%d" % b, [P, 4, P, 4], BF16) for b in range(2)]
+        w1q = [sbuf("w1q%d" % b, [P, 512], U32) for b in range(2)]
+        w1s = [sbuf("w1s%d" % b, [P, 512], U8) for b in range(2)]
+
+        def cast(copy, b, raw, m0, lo, n):
+            copy(
+                w1g[b][:, :, m0 + lo : m0 + lo + n, :].rearrange("p t m j -> p m j t"),
+                raw[:, :, 4 * lo : 4 * (lo + n)].rearrange("p j (m t) -> p m j t", t=4),
+            )
+
+        def quant_w1(b):
+            nc.vector.quantize_mx(w1q[b][:].bitcast(FP8X4), w1s[b][:], w1g[b][:].rearrange("p t m j -> p (t m j)"))
+
+        def w1_passes(b):
+            for jq in range(4):
+                for t in range(4):
+                    nc.tensor.matmul_mx(
+                        lin[b][jq][:, t, :],
+                        lhsT=w1q[b][:, P * t : P * (t + 1)].bitcast(FP8X4),
+                        lhsT_scale=w1s[b][:, P * t : P * (t + 1)],
+                        rhs=vw[0][:, P * jq : P * (jq + 1)].bitcast(FP8X4),
+                        rhs_scale=vs[PLANE[0] :, P * jq : P * (jq + 1)],
+                        start=False,
+                        stop=(t == 3),
+                    )
+
+        hb = [sbuf("hb%d" % b, [P, S, 4], BF16) for b in range(2)]
+        hq = [sbuf("hq%d" % b, [P, S], U32) for b in range(2)]
+        hs = [sbuf("hs%d" % b, [P, S], U8) for b in range(2)]
+
+        def relu(b, jq, on_scalar):
+            dst = hb[b][:, P * jq : P * (jq + 1), :]
+            src = lin[b][jq][:].rearrange("p t j -> p j t")
+            if on_scalar:
+                nc.scalar.activation(dst, src, ACT.Relu, bias=zero[:])
+            else:
+                nc.vector.tensor_scalar_max(dst, src, 0.0)
+
+        def quant_h(b, lo, n):
+            nc.vector.quantize_mx(
+                hq[b][:, lo : lo + n].bitcast(FP8X4),
+                hs[b][:, lo : lo + n],
+                hb[b][:, lo : lo + n, :].rearrange("p j t -> p (j t)"),
+            )
+
+        cast(nc.scalar.copy, 0, w1raw[0], 0, 0, 128)
+        v2s = [sbuf("v2s0", [P, 512], U8)]
+        gather2(v2s[0][:], tabs, 0, 512)
+        nc.vector.tensor_copy(vw[0][:], tabw[0][:].indirect(idx[:]))
+        quant_w1(0)
+        w1_passes(0)
+        v2w_11 = sbuf("v2w_11", [P, 512], U32, tag="w1g0")
+        gather2(v2w_11[:], tabw[1], 0, 512)
+        cast(nc.scalar.copy, 1, w1raw[1], 0, 0, 64)
+        cast(nc.scalar.copy, 1, w1raw[2], 64, 0, 24)
+        cast(nc.vector.tensor_copy, 1, w1raw[2], 64, 24, 40)
+        quant_w1(1)
+        w1_passes(1)
+        v2w_10 = sbuf("v2w_10", [P, 512], U32, tag="w1g1")
+        gather2(v2w_10[:], tabw[0], 0, 512)
+        for jq in range(4):
+            relu(0, jq, True)
+        relu(1, 0, False)
+        quant_h(0, 0, 512)
+        relu(1, 1, True)
+        relu(1, 2, False)
+        relu(1, 3, True)
+        quant_h(1, 0, 256)
+        quant_h(1, 256, 256)
+
+        ops = [[v[:, 256 * g : 256 * (g + 1)] for v in (v2s[0], v2w_10, v2w_11)] for g in range(2)] + [[], []]
+        holds = ["hb0", "hb1", "sq0", "sq1", "sq2", "sq3"]
+
+        def late_gather(i):
+            g, kind = 2 + i // 3, i % 3
+            dst = sbuf("late%d" % i, [P, 256], U32 if kind else U8, tag=holds[i])
+            gather2(dst[:], tabw[kind - 1] if kind else tabs, 256 * g, 256)
+            ops[g].append(dst[:])
+
+        late_gather(0)
+        late_gather(1)
+
+        for c in range(8):
+            g, cols = c // 2, slice(P * (c % 2), P * (c % 2 + 1))
+            e = bank(c, "e%d" % c, [P, S])
+            for a in range(2):
+                nc.tensor.matmul_mx(
+                    e[:],
+                    lhsT=ops[g][1 + a][:, cols].bitcast(FP8X4),
+                    lhsT_scale=ops[g][0][PLANE[a] :, cols],
+                    rhs=hq[a][:].bitcast(FP8X4),
+                    rhs_scale=hs[a][:],
+                    start=(a == 0),
+                    stop=(a == 1),
+                )
+            sq = sbuf("sq%d" % c, [P, S], F32)
+            nc.scalar.activation(sq[:], e[:], ACT.Square, bias=bias_col[:, c : c + 1])
+            sev = sbuf("sev%d" % c, [P, S], F32)
+            nc.vector.tensor_tensor(sev[:], sq[:], near_sb[c // 2][:, c % 2, :], ALU.add)
+            if c < 4:
+                late_gather(2 + c)
+            res = sbuf("res%d" % c, [P, S], F32)
+            nc.scalar.activation(res[:], sev[:], ACT.Sqrt, bias=zero[:])
+            nc.sync.dma_start(out[P * c : P * (c + 1), :], res[:])

@@ -22,7 +22,7 @@ S2 = 1024
 FLOPS = 2 * K * K * S + 2 * K * S2 * S
 
 PLANE = (12, 0)
-SCALE_LOADS = ((0, 12, 16), (12, 44, 0), (44, 68, 4), (68, 100, 0), (100, 128, 4))
+SCALE_LOADS = ((0, 4, 16), (12, 44, 0), (44, 68, 4), (68, 100, 0), (108, 112, 12))
 
 
 def tile_list_street_name_confusion_kernel(
@@ -31,6 +31,7 @@ def tile_list_street_name_confusion_kernel(
     nc = tc.nc
     with ExitStack() as ctx:
         sb = ctx.enter_context(tc.tile_pool(name="sb", bufs=1))
+        shared = ctx.enter_context(tc.tile_pool(name="shared", bufs=1))
         ps = ctx.enter_context(tc.psum_pool(name="ps", bufs=1))
 
         def sbuf(name, shape, dtype, tag=None):
@@ -44,7 +45,7 @@ def tile_list_street_name_confusion_kernel(
         tabw = [sbuf("tabw%d" % a, [P, T], U32) for a in range(2)]
         tabs = sbuf("tabs", [P, T], U8)
         w4raw = sbuf("w4raw", [P, 2 * K], U8)
-        w4sraw = sbuf("w4sraw", [P, K], U8)
+        w4sraw = shared.tile([P, K], U8, name="w4sraw", align_bytes=64, offset=1024)
         w1raw = [sbuf("w1raw0", [P, 4, 512], F32), sbuf("w1raw1", [P, 4, 256], F32), sbuf("w1raw2", [P, 4, 256], F32)]
         near_sb = [sbuf("near%d" % g, [P, 2, S], F32) for g in range(4)]
         bias_rows = sbuf("bias_rows", [P, P], F32)
@@ -52,52 +53,63 @@ def tile_list_street_name_confusion_kernel(
         zero_in = sbuf("zero_in", [P, 1], F32)
         zero = sbuf("zero", [P, 1], F32)
 
-        def load_words(a):
-            nc.sync.dma_start(tabw[a][:].bitcast(I32), tab_words[a].rearrange("p t i -> p (t i)").bitcast(I32))
+        def load_words(a, queue):
+            queue.dma_start(tabw[a][:].bitcast(I32), tab_words[a].rearrange("p t i -> p (t i)").bitcast(I32))
 
         w1v = w1.rearrange("(p j) c -> p j c", j=4)
         scale_rows = tab_scales.rearrange("a q t -> (a q) t").bitcast(I32)
 
-        nc.vector.memset(bias_rows[:], 0.0)
-        nc.scalar.dma_start(bias_rows[0:8, :], bias.rearrange("(c p) -> c p", p=P))
-        nc.vector.memset(w4sraw[:].bitcast(I32), 0)
-        nc.vector.memset(zero_in[:], 0.0)
-        load_words(1)
-        nc.sync.dma_start(w4raw[:].bitcast(I32), w4_words[0].bitcast(I32))
+        nc.gpsimd.memset(tabs[:].bitcast(I32), 0)
+        nc.gpsimd.memset(w4sraw[:].bitcast(I32), 0)
+        nc.gpsimd.memset(zero_in[:], 0.0)
+        nc.gpsimd.memset(bias_rows[:], 0.0)
+        nc.scalar.dma_start(w4raw[:].bitcast(I32), w4_words[0].bitcast(I32))
         nc.sync.dma_start(idx[:], offs)
-        for p0, p1, r0 in SCALE_LOADS:
-            nc.scalar.dma_start(tabs[p0:p1, :].bitcast(I32), scale_rows[r0 : r0 + p1 - p0, :])
-        for q in range(4):
-            nc.scalar.dma_start(w4sraw[32 * q : 32 * q + 4, :].bitcast(I32), w4_scales[0, 4 * q : 4 * q + 4, :].bitcast(I32))
-        nc.sync.dma_start(w1raw[0][:], w1v[:, :, 0:512])
+        load_words(1, nc.scalar)
         nc.sync.dma_start(idx2[:], offs2)
-        load_words(0)
+        for p0, p1, r0 in SCALE_LOADS:
+            nc.sync.dma_start(tabs[p0:p1, :].bitcast(I32), scale_rows[r0 : r0 + p1 - p0, :])
+        nc.sync.dma_start(w1raw[0][:], w1v[:, :, 0:512])
+        for q in range(4):
+            nc.sync.dma_start(w4sraw[32 * q : 32 * q + 4, :].bitcast(I32), w4_scales[0, 4 * q : 4 * q + 4, :].bitcast(I32))
         nc.sync.dma_start(w1raw[1][:], w1v[:, :, 512:768])
+        load_words(0, nc.sync)
         nc.sync.dma_start(w1raw[2][:], w1v[:, :, 768:1024])
+        nc.sync.dma_start(bias_rows[0:8, :], bias.rearrange("(c p) -> c p", p=P))
         for g in range(4):
             nc.sync.dma_start(near_sb[g][:], near[256 * g : 256 * (g + 1), :].rearrange("(c p) j -> p c j", p=P))
 
         nc.scalar.activation(zero[:], zero_in[:], ACT.Sqrt)
         make_identity(nc, ident[:])
-        bias_ps = bank(7, "bias_ps", [P, P])
-        nc.tensor.transpose(bias_ps[:], bias_rows[:], ident[:])
-        bias_col = sbuf("bias_col", [P, 8], F32)
-        nc.scalar.copy(bias_col[:], bias_ps[:, 0:8])
 
-        w4d = sbuf("w4d", [P, 4, 256, 2], U8)
-        w4sd = sbuf("w4sd", [P, 4, 256], U8)
-        nc.vector.tensor_copy(
-            w4d[:].rearrange("p t q e -> p q t e"), w4raw[:].rearrange("p (q t e) -> p q t e", t=4, e=2)
-        )
-        vw = [sbuf("vw%d" % a, [P, S], U32) for a in range(2)]
+        w4d = [sbuf("w4d%d" % b, [P, K], U8) for b in range(2)]
+        w4sd = [sbuf("w4sd%d" % b, [P, 512], U8) for b in range(2)]
+        vw = [None, sbuf("vw1", [P, S], U32)]
         vs = sbuf("vs", [P, S], U8)
 
         def gather2(dst, src, lo, n):
             nc.vector.tensor_copy(dst, src[:].indirect(idx2[:, lo // 16 : (lo + n) // 16]))
 
+        for b in range(2):
+            nc.vector.tensor_copy(
+                w4d[b][:].bitcast(U16).rearrange("p (t m) -> p m t", t=4),
+                w4raw[:, K * b : K * (b + 1)].bitcast(U16).rearrange("p (m t) -> p m t", t=4),
+            )
+        ops = [[None] * 3 for g in range(4)]
+
+        def gather_pairs(kind, g0, n, dst):
+            gather2(dst, tabw[kind - 1] if kind else tabs, 256 * g0, 256 * n)
+            for i in range(n):
+                ops[g0 + i][kind] = dst[:, 256 * i : 256 * (i + 1)]
+
         nc.vector.tensor_copy(vw[1][:], tabw[1][:].indirect(idx[:]))
         nc.vector.tensor_copy(vs[:], tabs[:].indirect(idx[:]))
-        nc.vector.tensor_copy(w4sd[:].rearrange("p t q -> p q t"), w4sraw[:].rearrange("p (q t) -> p q t", t=4))
+        gather_pairs(0, 0, 1, sbuf("v2s0", [P, 256], U8)[:])
+        for b in range(2):
+            nc.vector.tensor_copy(
+                w4sd[b][:].rearrange("p (t m) -> p m t", t=4),
+                w4sraw[:, 512 * b : 512 * (b + 1)].rearrange("p (m t) -> p m t", t=4),
+            )
 
         lin = [[bank(4 * b + jq, "lin%d%d" % (b, jq), [P, 4, P]) for jq in range(4)] for b in range(2)]
         for b in range(2):
@@ -105,8 +117,8 @@ def tile_list_street_name_confusion_kernel(
                 for jq in range(4):
                     nc.tensor.matmul_mx(
                         lin[b][jq][:, t, :],
-                        lhsT=w4d[:, t, P * b : P * (b + 1), :].rearrange("p q e -> p (q e)").bitcast(FP4X4),
-                        lhsT_scale=w4sd[:, t, P * b : P * (b + 1)],
+                        lhsT=w4d[b][:, 2 * P * t : 2 * P * (t + 1)].bitcast(FP4X4),
+                        lhsT_scale=w4sd[b][:, P * t : P * (t + 1)],
                         rhs=vw[1][:, P * jq : P * (jq + 1)].bitcast(FP8X4),
                         rhs_scale=vs[PLANE[1] :, P * jq : P * (jq + 1)],
                         start=(t == 0),
@@ -115,7 +127,7 @@ def tile_list_street_name_confusion_kernel(
 
         w1g = [sbuf("w1g%d" % b, [P, 4, P, 4], BF16) for b in range(2)]
         w1q = [sbuf("w1q%d" % b, [P, 512], U32) for b in range(2)]
-        w1s = [sbuf("w1s%d" % b, [P, 512], U8) for b in range(2)]
+        w1s = [shared.tile([P, 512], U8, name="w1s0", align_bytes=64, offset=1088), sbuf("w1s1", [P, 512], U8)]
 
         def cast(copy, b, raw, m0, lo, n):
             copy(
@@ -123,12 +135,16 @@ def tile_list_street_name_confusion_kernel(
                 raw[:, :, 4 * lo : 4 * (lo + n)].rearrange("p j (m t) -> p m j t", t=4),
             )
 
-        def quant_w1(b):
-            nc.vector.quantize_mx(w1q[b][:].bitcast(FP8X4), w1s[b][:], w1g[b][:].rearrange("p t m j -> p (t m j)"))
+        def quant_w1(b, t0, t1):
+            nc.vector.quantize_mx(
+                w1q[b][:, P * t0 : P * t1].bitcast(FP8X4),
+                w1s[b][:, P * t0 : P * t1],
+                w1g[b][:, t0:t1, :, :].rearrange("p t m j -> p (t m j)"),
+            )
 
-        def w1_passes(b):
+        def w1_passes(b, t0, t1):
             for jq in range(4):
-                for t in range(4):
+                for t in range(t0, t1):
                     nc.tensor.matmul_mx(
                         lin[b][jq][:, t, :],
                         lhsT=w1q[b][:, P * t : P * (t + 1)].bitcast(FP8X4),
@@ -139,7 +155,7 @@ def tile_list_street_name_confusion_kernel(
                         stop=(t == 3),
                     )
 
-        hb = [sbuf("hb%d" % b, [P, S, 4], BF16) for b in range(2)]
+        hb = [None, shared.tile([P, S, 4], BF16, name="hb1", align_bytes=64, offset=4096)]
         hq = [sbuf("hq%d" % b, [P, S], U32) for b in range(2)]
         hs = [sbuf("hs%d" % b, [P, S], U8) for b in range(2)]
 
@@ -159,41 +175,50 @@ def tile_list_street_name_confusion_kernel(
             )
 
         cast(nc.scalar.copy, 0, w1raw[0], 0, 0, 128)
-        v2s = [sbuf("v2s0", [P, 512], U8)]
-        gather2(v2s[0][:], tabs, 0, 512)
-        nc.vector.tensor_copy(vw[0][:], tabw[0][:].indirect(idx[:]))
-        quant_w1(0)
-        w1_passes(0)
-        v2w_11 = sbuf("v2w_11", [P, 512], U32, tag="w1g0")
-        gather2(v2w_11[:], tabw[1], 0, 512)
+        gather_pairs(0, 1, 2, shared.tile([P, 512], U8, name="v2s1", align_bytes=64, offset=1600)[:])
+        quant_w1(0, 0, 4)
+        gather_pairs(2, 0, 1, shared.tile([P, 256], U32, name="v2w10", align_bytes=64, offset=64)[:])
+        vw[0] = sbuf("vw0", [P, S], U32)
+        for h in range(2):
+            nc.vector.tensor_copy(vw[0][:, 256 * h : 256 * (h + 1)], tabw[0][:].indirect(idx[:, 16 * h : 16 * (h + 1)]))
+        w1_passes(0, 0, 4)
         cast(nc.scalar.copy, 1, w1raw[1], 0, 0, 64)
-        cast(nc.scalar.copy, 1, w1raw[2], 64, 0, 24)
-        cast(nc.vector.tensor_copy, 1, w1raw[2], 64, 24, 40)
-        quant_w1(1)
-        w1_passes(1)
-        v2w_10 = sbuf("v2w_10", [P, 512], U32, tag="w1g1")
-        gather2(v2w_10[:], tabw[0], 0, 512)
+        cast(nc.vector.tensor_copy, 1, w1raw[2], 64, 0, 64)
+        for t0 in (0, 2):
+            quant_w1(1, t0, t0 + 2)
+            w1_passes(1, t0, t0 + 2)
+        gather_pairs(1, 0, 1, sbuf("v2w00", [P, 256], U32, tag="w1g1")[:])
+        hb[0] = sbuf("hb0", [P, S, 4], BF16, tag="w1raw1")
         for jq in range(4):
             relu(0, jq, True)
-        relu(1, 0, False)
+        bias_ps = bank(0, "bias_ps", [P, P])
+        nc.tensor.transpose(bias_ps[:], bias_rows[:], ident[:])
+        bias_col = sbuf("bias_col", [P, 8], F32, tag="w1raw2")
+        nc.vector.tensor_copy(bias_col[:], bias_ps[:, 0:8])
         quant_h(0, 0, 512)
+        relu(1, 0, True)
         relu(1, 1, True)
         relu(1, 2, False)
         relu(1, 3, True)
         quant_h(1, 0, 256)
-        quant_h(1, 256, 256)
+        quant_h(1, 256, 128)
+        quant_h(1, 384, 128)
 
-        ops = [[v[:, 256 * g : 256 * (g + 1)] for v in (v2s[0], v2w_10, v2w_11)] for g in range(2)] + [[], []]
-        holds = ["hb0", "hb1", "sq0", "sq1", "sq2", "sq3"]
+        late_s = shared.tile([P, 256], U8, name="late_s", align_bytes=64, offset=4096)
+        late_w = shared.tile([P, 6 * 256], U32, name="late_w", align_bytes=64, offset=4096 + 256)
+        for g in range(1, 4):
+            if g == 3:
+                gather_pairs(0, g, 1, late_s[:])
+            for a in range(2):
+                i = 2 * (g - 1) + a
+                gather_pairs(1 + a, g, 1, late_w[:, 256 * i : 256 * (i + 1)])
 
-        def late_gather(i):
-            g, kind = 2 + i // 3, i % 3
-            dst = sbuf("late%d" % i, [P, 256], U32 if kind else U8, tag=holds[i])
-            gather2(dst[:], tabw[kind - 1] if kind else tabs, 256 * g, 256)
-            ops[g].append(dst[:])
+        sev = []
 
-        late_gather(0)
-        late_gather(1)
+        def root(c):
+            res = sbuf("res%d" % c, [P, S], F32)
+            nc.scalar.activation(res[:], sev[c][:], ACT.Sqrt, bias=zero[:])
+            nc.sync.dma_start(out[P * c : P * (c + 1), :], res[:])
 
         for c in range(8):
             g, cols = c // 2, slice(P * (c % 2), P * (c % 2 + 1))
@@ -210,10 +235,10 @@ def tile_list_street_name_confusion_kernel(
                 )
             sq = sbuf("sq%d" % c, [P, S], F32)
             nc.scalar.activation(sq[:], e[:], ACT.Square, bias=bias_col[:, c : c + 1])
-            sev = sbuf("sev%d" % c, [P, S], F32)
-            nc.vector.tensor_tensor(sev[:], sq[:], near_sb[c // 2][:, c % 2, :], ALU.add)
-            if c < 4:
-                late_gather(2 + c)
-            res = sbuf("res%d" % c, [P, S], F32)
-            nc.scalar.activation(res[:], sev[:], ACT.Sqrt, bias=zero[:])
-            nc.sync.dma_start(out[P * c : P * (c + 1), :], res[:])
+            sev.append(sbuf("sev%d" % c, [P, S], F32))
+            adder = nc.gpsimd if c < 3 else nc.vector
+            adder.tensor_tensor(sev[c][:], sq[:], near_sb[c // 2][:, c % 2, :], ALU.add)
+            if c >= 2:
+                root(c - 2)
+        root(6)
+        root(7)

@@ -16,13 +16,25 @@ ALU = mybir.AluOpType
 
 P = 128
 K = 1024
+PASS = 512
 T = 2048
 S = 512
 S2 = 1024
+PER_COL = 16
+PIECE = 256
 FLOPS = 2 * K * K * S + 2 * K * S2 * S
 
 PLANE = (12, 0)
 SCALE_LOADS = ((0, 4, 16), (12, 44, 0), (44, 68, 4), (68, 100, 0), (108, 112, 12))
+
+SCALES, WORDS0, WORDS1 = 0, 1, 2
+
+W4S_AT = 1024
+AFTER_W4S = (64, 1088, 1600)
+HB1_AT = 4096
+
+GPSIMD_ADDS = 3
+VECTOR_SQUARE = 5
 
 
 def tile_list_street_name_confusion_kernel(
@@ -37,15 +49,18 @@ def tile_list_street_name_confusion_kernel(
         def sbuf(name, shape, dtype, tag=None):
             return sb.tile(shape, dtype, name=name, tag=tag or name, align_bytes=64)
 
+        def placed(name, shape, dtype, offset):
+            return shared.tile(shape, dtype, name=name, align_bytes=64, offset=offset)
+
         def bank(i, name, shape):
             return ps.tile(shape, F32, name=name, tag="bank%d" % i)
 
-        idx = sb.tile([P, S // 16], U16, name="idx")
-        idx2 = sb.tile([P, S2 // 16], U16, name="idx2")
+        idx = sb.tile([P, S // PER_COL], U16, name="idx")
+        idx2 = sb.tile([P, S2 // PER_COL], U16, name="idx2")
         tabw = [sbuf("tabw%d" % a, [P, T], U32) for a in range(2)]
         tabs = sbuf("tabs", [P, T], U8)
         w4raw = sbuf("w4raw", [P, 2 * K], U8)
-        w4sraw = shared.tile([P, K], U8, name="w4sraw", align_bytes=64, offset=1024)
+        w4sraw = placed("w4sraw", [P, K], U8, W4S_AT)
         w1raw = [sbuf("w1raw0", [P, 4, 512], F32), sbuf("w1raw1", [P, 4, 256], F32), sbuf("w1raw2", [P, 4, 256], F32)]
         near_sb = [sbuf("near%d" % g, [P, 2, S], F32) for g in range(4)]
         bias_rows = sbuf("bias_rows", [P, P], F32)
@@ -77,39 +92,37 @@ def tile_list_street_name_confusion_kernel(
         nc.sync.dma_start(w1raw[2][:], w1v[:, :, 768:1024])
         nc.sync.dma_start(bias_rows[0:8, :], bias.rearrange("(c p) -> c p", p=P))
         for g in range(4):
-            nc.sync.dma_start(near_sb[g][:], near[256 * g : 256 * (g + 1), :].rearrange("(c p) j -> p c j", p=P))
+            nc.sync.dma_start(near_sb[g][:], near[PIECE * g : PIECE * (g + 1), :].rearrange("(c p) j -> p c j", p=P))
 
         nc.scalar.activation(zero[:], zero_in[:], ACT.Sqrt)
         make_identity(nc, ident[:])
 
         w4d = [sbuf("w4d%d" % b, [P, K], U8) for b in range(2)]
-        w4sd = [sbuf("w4sd%d" % b, [P, 512], U8) for b in range(2)]
+        w4sd = [sbuf("w4sd%d" % b, [P, PASS], U8) for b in range(2)]
         vw = [None, sbuf("vw1", [P, S], U32)]
         vs = sbuf("vs", [P, S], U8)
 
-        def gather2(dst, src, lo, n):
-            nc.vector.tensor_copy(dst, src[:].indirect(idx2[:, lo // 16 : (lo + n) // 16]))
-
-        for b in range(2):
+        def deal(dst, src, run):
             nc.vector.tensor_copy(
-                w4d[b][:].bitcast(U16).rearrange("p (t m) -> p m t", t=4),
-                w4raw[:, K * b : K * (b + 1)].bitcast(U16).rearrange("p (m t) -> p m t", t=4),
+                dst.rearrange("p (t r i) -> p r t i", t=4, i=run), src.rearrange("p (r i t) -> p r t i", t=4, i=run)
             )
-        ops = [[None] * 3 for g in range(4)]
+
+        v2 = [[None] * 3 for g in range(S2 // PIECE)]
 
         def gather_pairs(kind, g0, n, dst):
-            gather2(dst, tabw[kind - 1] if kind else tabs, 256 * g0, 256 * n)
+            window = tabs if kind == SCALES else tabw[kind - WORDS0]
+            entries = idx2[:, PIECE * g0 // PER_COL : PIECE * (g0 + n) // PER_COL]
+            nc.vector.tensor_copy(dst, window[:].indirect(entries))
             for i in range(n):
-                ops[g0 + i][kind] = dst[:, 256 * i : 256 * (i + 1)]
+                v2[g0 + i][kind] = dst[:, PIECE * i : PIECE * (i + 1)]
 
+        for b in range(2):
+            deal(w4d[b][:].bitcast(U16), w4raw[:, K * b : K * (b + 1)].bitcast(U16), 8)
         nc.vector.tensor_copy(vw[1][:], tabw[1][:].indirect(idx[:]))
         nc.vector.tensor_copy(vs[:], tabs[:].indirect(idx[:]))
-        gather_pairs(0, 0, 1, sbuf("v2s0", [P, 256], U8)[:])
+        gather_pairs(SCALES, 0, 1, sbuf("v2s0", [P, PIECE], U8)[:])
         for b in range(2):
-            nc.vector.tensor_copy(
-                w4sd[b][:].rearrange("p (t m) -> p m t", t=4),
-                w4sraw[:, 512 * b : 512 * (b + 1)].rearrange("p (m t) -> p m t", t=4),
-            )
+            deal(w4sd[b][:], w4sraw[:, PASS * b : PASS * (b + 1)], 16)
 
         lin = [[bank(4 * b + jq, "lin%d%d" % (b, jq), [P, 4, P]) for jq in range(4)] for b in range(2)]
         for b in range(2):
@@ -126,13 +139,13 @@ def tile_list_street_name_confusion_kernel(
                     )
 
         w1g = [sbuf("w1g%d" % b, [P, 4, P, 4], BF16) for b in range(2)]
-        w1q = [sbuf("w1q%d" % b, [P, 512], U32) for b in range(2)]
-        w1s = [shared.tile([P, 512], U8, name="w1s0", align_bytes=64, offset=1088), sbuf("w1s1", [P, 512], U8)]
+        w1q = [sbuf("w1q%d" % b, [P, PASS], U32) for b in range(2)]
+        w1s = [placed("w1s0", [P, PASS], U8, AFTER_W4S[1]), sbuf("w1s1", [P, PASS], U8)]
 
-        def cast(copy, b, raw, m0, lo, n):
+        def cast(copy, b, raw, m0):
             copy(
-                w1g[b][:, :, m0 + lo : m0 + lo + n, :].rearrange("p t m j -> p m j t"),
-                raw[:, :, 4 * lo : 4 * (lo + n)].rearrange("p j (m t) -> p m j t", t=4),
+                w1g[b][:, :, m0 : m0 + raw.shape[2] // 4, :].rearrange("p t m j -> p m t j"),
+                raw[:].rearrange("p j (m t) -> p m t j", t=4),
             )
 
         def quant_w1(b, t0, t1):
@@ -155,7 +168,7 @@ def tile_list_street_name_confusion_kernel(
                         stop=(t == 3),
                     )
 
-        hb = [None, shared.tile([P, S, 4], BF16, name="hb1", align_bytes=64, offset=4096)]
+        hb = [None, placed("hb1", [P, S, 4], BF16, HB1_AT)]
         hq = [sbuf("hq%d" % b, [P, S], U32) for b in range(2)]
         hs = [sbuf("hs%d" % b, [P, S], U8) for b in range(2)]
 
@@ -174,71 +187,76 @@ def tile_list_street_name_confusion_kernel(
                 hb[b][:, lo : lo + n, :].rearrange("p j t -> p (j t)"),
             )
 
-        cast(nc.scalar.copy, 0, w1raw[0], 0, 0, 128)
-        gather_pairs(0, 1, 2, shared.tile([P, 512], U8, name="v2s1", align_bytes=64, offset=1600)[:])
+        cast(nc.scalar.copy, 0, w1raw[0], 0)
+        gather_pairs(SCALES, 1, 2, placed("v2s1", [P, 2 * PIECE], U8, AFTER_W4S[2])[:])
         quant_w1(0, 0, 4)
-        gather_pairs(2, 0, 1, shared.tile([P, 256], U32, name="v2w10", align_bytes=64, offset=64)[:])
+        gather_pairs(WORDS1, 0, 1, placed("v2w10", [P, PIECE], U32, AFTER_W4S[0])[:])
         vw[0] = sbuf("vw0", [P, S], U32)
-        for h in range(2):
-            nc.vector.tensor_copy(vw[0][:, 256 * h : 256 * (h + 1)], tabw[0][:].indirect(idx[:, 16 * h : 16 * (h + 1)]))
+        for lo in range(0, S, PIECE):
+            entries = idx[:, lo // PER_COL : (lo + PIECE) // PER_COL]
+            nc.vector.tensor_copy(vw[0][:, lo : lo + PIECE], tabw[0][:].indirect(entries))
         w1_passes(0, 0, 4)
-        cast(nc.scalar.copy, 1, w1raw[1], 0, 0, 64)
-        cast(nc.vector.tensor_copy, 1, w1raw[2], 64, 0, 64)
+        cast(nc.scalar.copy, 1, w1raw[1], 0)
+        cast(nc.vector.tensor_copy, 1, w1raw[2], P // 2)
         for t0 in (0, 2):
             quant_w1(1, t0, t0 + 2)
             w1_passes(1, t0, t0 + 2)
-        gather_pairs(1, 0, 1, sbuf("v2w00", [P, 256], U32, tag="w1g1")[:])
+        gather_pairs(WORDS0, 0, 1, sbuf("v2w00", [P, PIECE], U32, tag="w1g1")[:])
         hb[0] = sbuf("hb0", [P, S, 4], BF16, tag="w1raw1")
         for jq in range(4):
             relu(0, jq, True)
         bias_ps = bank(0, "bias_ps", [P, P])
         nc.tensor.transpose(bias_ps[:], bias_rows[:], ident[:])
-        bias_col = sbuf("bias_col", [P, 8], F32, tag="w1raw2")
-        nc.vector.tensor_copy(bias_col[:], bias_ps[:, 0:8])
-        quant_h(0, 0, 512)
-        relu(1, 0, True)
-        relu(1, 1, True)
-        relu(1, 2, False)
-        relu(1, 3, True)
-        quant_h(1, 0, 256)
-        quant_h(1, 256, 128)
-        quant_h(1, 384, 128)
+        bias_col = sbuf("bias_col", [P, S2 // P], F32, tag="w1raw2")
+        nc.vector.tensor_copy(bias_col[:], bias_ps[:, 0 : S2 // P])
+        quant_h(0, 0, S)
+        for jq in range(4):
+            relu(1, jq, jq != 2)
+        for lo, n in ((0, 2 * P), (2 * P, P), (3 * P, P)):
+            quant_h(1, lo, n)
 
-        late_s = shared.tile([P, 256], U8, name="late_s", align_bytes=64, offset=4096)
-        late_w = shared.tile([P, 6 * 256], U32, name="late_w", align_bytes=64, offset=4096 + 256)
+        late_s = placed("late_s", [P, PIECE], U8, HB1_AT)
+        late_w = placed("late_w", [P, 6 * PIECE], U32, HB1_AT + PIECE)
         for g in range(1, 4):
-            if g == 3:
-                gather_pairs(0, g, 1, late_s[:])
+            if v2[g][SCALES] is None:
+                gather_pairs(SCALES, g, 1, late_s[:])
             for a in range(2):
                 i = 2 * (g - 1) + a
-                gather_pairs(1 + a, g, 1, late_w[:, 256 * i : 256 * (i + 1)])
+                gather_pairs(WORDS0 + a, g, 1, late_w[:, PIECE * i : PIECE * (i + 1)])
 
         sev = []
+        rooted = []
 
-        def root(c):
-            res = sbuf("res%d" % c, [P, S], F32)
-            nc.scalar.activation(res[:], sev[c][:], ACT.Sqrt, bias=zero[:])
-            nc.sync.dma_start(out[P * c : P * (c + 1), :], res[:])
+        def root():
+            c = len(rooted)
+            rooted.append(sbuf("res%d" % c, [P, S], F32))
+            nc.scalar.activation(rooted[c][:], sev[c][:], ACT.Sqrt, bias=zero[:])
+            nc.sync.dma_start(out[P * c : P * (c + 1), :], rooted[c][:])
 
-        for c in range(8):
+        for c in range(S2 // P):
             g, cols = c // 2, slice(P * (c % 2), P * (c % 2 + 1))
             e = bank(c, "e%d" % c, [P, S])
             for a in range(2):
                 nc.tensor.matmul_mx(
                     e[:],
-                    lhsT=ops[g][1 + a][:, cols].bitcast(FP8X4),
-                    lhsT_scale=ops[g][0][PLANE[a] :, cols],
+                    lhsT=v2[g][WORDS0 + a][:, cols].bitcast(FP8X4),
+                    lhsT_scale=v2[g][SCALES][PLANE[a] :, cols],
                     rhs=hq[a][:].bitcast(FP8X4),
                     rhs_scale=hs[a][:],
                     start=(a == 0),
                     stop=(a == 1),
                 )
             sq = sbuf("sq%d" % c, [P, S], F32)
-            nc.scalar.activation(sq[:], e[:], ACT.Square, bias=bias_col[:, c : c + 1])
+            if c == VECTOR_SQUARE:
+                shifted = sbuf("shifted", [P, S], F32)
+                nc.vector.tensor_scalar_add(shifted[:], e[:], bias_col[:, c : c + 1])
+                nc.vector.scalar_tensor_tensor(sq[:], e[:], bias_col[:, c : c + 1], shifted[:], ALU.add, ALU.mult)
+            else:
+                nc.scalar.activation(sq[:], e[:], ACT.Square, bias=bias_col[:, c : c + 1])
             sev.append(sbuf("sev%d" % c, [P, S], F32))
-            adder = nc.gpsimd if c < 3 else nc.vector
-            adder.tensor_tensor(sev[c][:], sq[:], near_sb[c // 2][:, c % 2, :], ALU.add)
-            if c >= 2:
-                root(c - 2)
-        root(6)
-        root(7)
+            adder = nc.gpsimd if c < GPSIMD_ADDS else nc.vector
+            adder.tensor_tensor(sev[c][:], sq[:], near_sb[g][:, c % 2, :], ALU.add)
+            if c >= 2 and c != VECTOR_SQUARE:
+                root()
+        for c in range(len(rooted), S2 // P):
+            root()

from contextlib import ExitStack

import concourse.mybir as mybir
from concourse.masks import make_identity

F32 = mybir.dt.float32
BF16 = mybir.dt.bfloat16
I32 = mybir.dt.int32
U32 = mybir.dt.uint32
U16 = mybir.dt.uint16
U8 = mybir.dt.uint8
FP8X4 = mybir.dt.float8_e4m3fn_x4
FP4X4 = mybir.dt.float4_e2m1fn_x4
ACT = mybir.ActivationFunctionType
ALU = mybir.AluOpType

P = 128
K = 1024
PASS = 512
T = 2048
S = 512
S2 = 1024
PER_COL = 16
PIECE = 256
FLOPS = 2 * K * K * S + 2 * K * S2 * S

PLANE = (12, 0)
SCALE_LOADS = ((0, 4, 16), (12, 44, 0), (44, 68, 4), (68, 100, 0), (108, 112, 12))

SCALES, WORDS0, WORDS1 = 0, 1, 2

W4S_AT = 1024
AFTER_W4S = (64, 1088, 1600)
HB1_AT = 4096

GPSIMD_ADDS = 3
VECTOR_SQUARE = 5


def tile_list_street_name_confusion_kernel(
    tc, tab_words, tab_scales, offs, offs2, w1, w4_words, w4_scales, bias, near, out
):
    nc = tc.nc
    with ExitStack() as ctx:
        sb = ctx.enter_context(tc.tile_pool(name="sb", bufs=1))
        shared = ctx.enter_context(tc.tile_pool(name="shared", bufs=1))
        ps = ctx.enter_context(tc.psum_pool(name="ps", bufs=1))

        def sbuf(name, shape, dtype, tag=None):
            return sb.tile(shape, dtype, name=name, tag=tag or name, align_bytes=64)

        def placed(name, shape, dtype, offset):
            return shared.tile(shape, dtype, name=name, align_bytes=64, offset=offset)

        def bank(i, name, shape):
            return ps.tile(shape, F32, name=name, tag="bank%d" % i)

        idx = sb.tile([P, S // PER_COL], U16, name="idx")
        idx2 = sb.tile([P, S2 // PER_COL], U16, name="idx2")
        tabw = [sbuf("tabw%d" % a, [P, T], U32) for a in range(2)]
        tabs = sbuf("tabs", [P, T], U8)
        w4raw = sbuf("w4raw", [P, 2 * K], U8)
        w4sraw = placed("w4sraw", [P, K], U8, W4S_AT)
        w1raw = [sbuf("w1raw0", [P, 4, 512], F32), sbuf("w1raw1", [P, 4, 256], F32), sbuf("w1raw2", [P, 4, 256], F32)]
        near_sb = [sbuf("near%d" % g, [P, 2, S], F32) for g in range(4)]
        bias_rows = sbuf("bias_rows", [P, P], F32)
        ident = sbuf("ident", [P, P], F32)
        zero_in = sbuf("zero_in", [P, 1], F32)
        zero = sbuf("zero", [P, 1], F32)

        def load_words(a, queue):
            queue.dma_start(tabw[a][:].bitcast(I32), tab_words[a].rearrange("p t i -> p (t i)").bitcast(I32))

        w1v = w1.rearrange("(p j) c -> p j c", j=4)
        scale_rows = tab_scales.rearrange("a q t -> (a q) t").bitcast(I32)

        nc.gpsimd.memset(tabs[:].bitcast(I32), 0)
        nc.gpsimd.memset(w4sraw[:].bitcast(I32), 0)
        nc.gpsimd.memset(zero_in[:], 0.0)
        nc.gpsimd.memset(bias_rows[:], 0.0)
        nc.scalar.dma_start(w4raw[:].bitcast(I32), w4_words[0].bitcast(I32))
        nc.sync.dma_start(idx[:], offs)
        load_words(1, nc.scalar)
        nc.sync.dma_start(idx2[:], offs2)
        for p0, p1, r0 in SCALE_LOADS:
            nc.sync.dma_start(tabs[p0:p1, :].bitcast(I32), scale_rows[r0 : r0 + p1 - p0, :])
        nc.sync.dma_start(w1raw[0][:], w1v[:, :, 0:512])
        for q in range(4):
            nc.sync.dma_start(w4sraw[32 * q : 32 * q + 4, :].bitcast(I32), w4_scales[0, 4 * q : 4 * q + 4, :].bitcast(I32))
        nc.sync.dma_start(w1raw[1][:], w1v[:, :, 512:768])
        load_words(0, nc.sync)
        nc.sync.dma_start(w1raw[2][:], w1v[:, :, 768:1024])
        nc.sync.dma_start(bias_rows[0:8, :], bias.rearrange("(c p) -> c p", p=P))
        for g in range(4):
            nc.sync.dma_start(near_sb[g][:], near[PIECE * g : PIECE * (g + 1), :].rearrange("(c p) j -> p c j", p=P))

        nc.scalar.activation(zero[:], zero_in[:], ACT.Sqrt)
        make_identity(nc, ident[:])

        w4d = [sbuf("w4d%d" % b, [P, K], U8) for b in range(2)]
        w4sd = [sbuf("w4sd%d" % b, [P, PASS], U8) for b in range(2)]
        vw = [None, sbuf("vw1", [P, S], U32)]
        vs = sbuf("vs", [P, S], U8)

        def deal(dst, src, run):
            nc.vector.tensor_copy(
                dst.rearrange("p (t r i) -> p r t i", t=4, i=run), src.rearrange("p (r i t) -> p r t i", t=4, i=run)
            )

        v2 = [[None] * 3 for g in range(S2 // PIECE)]

        def gather_pairs(kind, g0, n, dst):
            window = tabs if kind == SCALES else tabw[kind - WORDS0]
            entries = idx2[:, PIECE * g0 // PER_COL : PIECE * (g0 + n) // PER_COL]
            nc.vector.tensor_copy(dst, window[:].indirect(entries))
            for i in range(n):
                v2[g0 + i][kind] = dst[:, PIECE * i : PIECE * (i + 1)]

        for b in range(2):
            deal(w4d[b][:].bitcast(U16), w4raw[:, K * b : K * (b + 1)].bitcast(U16), 8)
        nc.vector.tensor_copy(vw[1][:], tabw[1][:].indirect(idx[:]))
        nc.vector.tensor_copy(vs[:], tabs[:].indirect(idx[:]))
        gather_pairs(SCALES, 0, 1, sbuf("v2s0", [P, PIECE], U8)[:])
        for b in range(2):
            deal(w4sd[b][:], w4sraw[:, PASS * b : PASS * (b + 1)], 16)

        lin = [[bank(4 * b + jq, "lin%d%d" % (b, jq), [P, 4, P]) for jq in range(4)] for b in range(2)]
        for b in range(2):
            for t in range(4):
                for jq in range(4):
                    nc.tensor.matmul_mx(
                        lin[b][jq][:, t, :],
                        lhsT=w4d[b][:, 2 * P * t : 2 * P * (t + 1)].bitcast(FP4X4),
                        lhsT_scale=w4sd[b][:, P * t : P * (t + 1)],
                        rhs=vw[1][:, P * jq : P * (jq + 1)].bitcast(FP8X4),
                        rhs_scale=vs[PLANE[1] :, P * jq : P * (jq + 1)],
                        start=(t == 0),
                        stop=False,
                    )

        w1g = [sbuf("w1g%d" % b, [P, 4, P, 4], BF16) for b in range(2)]
        w1q = [sbuf("w1q%d" % b, [P, PASS], U32) for b in range(2)]
        w1s = [placed("w1s0", [P, PASS], U8, AFTER_W4S[1]), sbuf("w1s1", [P, PASS], U8)]

        def cast(copy, b, raw, m0):
            copy(
                w1g[b][:, :, m0 : m0 + raw.shape[2] // 4, :].rearrange("p t m j -> p m t j"),
                raw[:].rearrange("p j (m t) -> p m t j", t=4),
            )

        def quant_w1(b, t0, t1):
            nc.vector.quantize_mx(
                w1q[b][:, P * t0 : P * t1].bitcast(FP8X4),
                w1s[b][:, P * t0 : P * t1],
                w1g[b][:, t0:t1, :, :].rearrange("p t m j -> p (t m j)"),
            )

        def w1_passes(b, t0, t1):
            for jq in range(4):
                for t in range(t0, t1):
                    nc.tensor.matmul_mx(
                        lin[b][jq][:, t, :],
                        lhsT=w1q[b][:, P * t : P * (t + 1)].bitcast(FP8X4),
                        lhsT_scale=w1s[b][:, P * t : P * (t + 1)],
                        rhs=vw[0][:, P * jq : P * (jq + 1)].bitcast(FP8X4),
                        rhs_scale=vs[PLANE[0] :, P * jq : P * (jq + 1)],
                        start=False,
                        stop=(t == 3),
                    )

        hb = [None, placed("hb1", [P, S, 4], BF16, HB1_AT)]
        hq = [sbuf("hq%d" % b, [P, S], U32) for b in range(2)]
        hs = [sbuf("hs%d" % b, [P, S], U8) for b in range(2)]

        def relu(b, jq, on_scalar):
            dst = hb[b][:, P * jq : P * (jq + 1), :]
            src = lin[b][jq][:].rearrange("p t j -> p j t")
            if on_scalar:
                nc.scalar.activation(dst, src, ACT.Relu, bias=zero[:])
            else:
                nc.vector.tensor_scalar_max(dst, src, 0.0)

        def quant_h(b, lo, n):
            nc.vector.quantize_mx(
                hq[b][:, lo : lo + n].bitcast(FP8X4),
                hs[b][:, lo : lo + n],
                hb[b][:, lo : lo + n, :].rearrange("p j t -> p (j t)"),
            )

        cast(nc.scalar.copy, 0, w1raw[0], 0)
        gather_pairs(SCALES, 1, 2, placed("v2s1", [P, 2 * PIECE], U8, AFTER_W4S[2])[:])
        quant_w1(0, 0, 4)
        gather_pairs(WORDS1, 0, 1, placed("v2w10", [P, PIECE], U32, AFTER_W4S[0])[:])
        vw[0] = sbuf("vw0", [P, S], U32)
        for lo in range(0, S, PIECE):
            entries = idx[:, lo // PER_COL : (lo + PIECE) // PER_COL]
            nc.vector.tensor_copy(vw[0][:, lo : lo + PIECE], tabw[0][:].indirect(entries))
        w1_passes(0, 0, 4)
        cast(nc.scalar.copy, 1, w1raw[1], 0)
        cast(nc.vector.tensor_copy, 1, w1raw[2], P // 2)
        for t0 in (0, 2):
            quant_w1(1, t0, t0 + 2)
            w1_passes(1, t0, t0 + 2)
        gather_pairs(WORDS0, 0, 1, sbuf("v2w00", [P, PIECE], U32, tag="w1g1")[:])
        hb[0] = sbuf("hb0", [P, S, 4], BF16, tag="w1raw1")
        for jq in range(4):
            relu(0, jq, True)
        bias_ps = bank(0, "bias_ps", [P, P])
        nc.tensor.transpose(bias_ps[:], bias_rows[:], ident[:])
        bias_col = sbuf("bias_col", [P, S2 // P], F32, tag="w1raw2")
        nc.vector.tensor_copy(bias_col[:], bias_ps[:, 0 : S2 // P])
        quant_h(0, 0, S)
        for jq in range(4):
            relu(1, jq, jq != 2)
        for lo, n in ((0, 2 * P), (2 * P, P), (3 * P, P)):
            quant_h(1, lo, n)

        late_s = placed("late_s", [P, PIECE], U8, HB1_AT)
        late_w = placed("late_w", [P, 6 * PIECE], U32, HB1_AT + PIECE)
        for g in range(1, 4):
            if v2[g][SCALES] is None:
                gather_pairs(SCALES, g, 1, late_s[:])
            for a in range(2):
                i = 2 * (g - 1) + a
                gather_pairs(WORDS0 + a, g, 1, late_w[:, PIECE * i : PIECE * (i + 1)])

        sev = []
        rooted = []

        def root():
            c = len(rooted)
            rooted.append(sbuf("res%d" % c, [P, S], F32))
            nc.scalar.activation(rooted[c][:], sev[c][:], ACT.Sqrt, bias=zero[:])
            nc.sync.dma_start(out[P * c : P * (c + 1), :], rooted[c][:])

        for c in range(S2 // P):
            g, cols = c // 2, slice(P * (c % 2), P * (c % 2 + 1))
            e = bank(c, "e%d" % c, [P, S])
            for a in range(2):
                nc.tensor.matmul_mx(
                    e[:],
                    lhsT=v2[g][WORDS0 + a][:, cols].bitcast(FP8X4),
                    lhsT_scale=v2[g][SCALES][PLANE[a] :, cols],
                    rhs=hq[a][:].bitcast(FP8X4),
                    rhs_scale=hs[a][:],
                    start=(a == 0),
                    stop=(a == 1),
                )
            sq = sbuf("sq%d" % c, [P, S], F32)
            if c == VECTOR_SQUARE:
                shifted = sbuf("shifted", [P, S], F32)
                nc.vector.tensor_scalar_add(shifted[:], e[:], bias_col[:, c : c + 1])
                nc.vector.scalar_tensor_tensor(sq[:], e[:], bias_col[:, c : c + 1], shifted[:], ALU.add, ALU.mult)
            else:
                nc.scalar.activation(sq[:], e[:], ACT.Square, bias=bias_col[:, c : c + 1])
            sev.append(sbuf("sev%d" % c, [P, S], F32))
            adder = nc.gpsimd if c < GPSIMD_ADDS else nc.vector
            adder.tensor_tensor(sev[c][:], sq[:], near_sb[g][:, c % 2, :], ALU.add)
            if c >= 2 and c != VECTOR_SQUARE:
                root()
        for c in range(len(rooted), S2 // P):
            root()
